import numpy as np
import ml_dtypes


def mxq(x, axis, fmt="e4m3"):
    dtype, down = {"e4m3": (ml_dtypes.float8_e4m3fn, 7), "e5m2": (ml_dtypes.float8_e5m2, 14)}[fmt]
    v = np.moveaxis(np.asarray(x, np.float32).astype(ml_dtypes.bfloat16).astype(np.float64), axis, -1)
    blocks = v.reshape(v.shape[:-1] + (-1, 32))
    amax = np.abs(blocks).max(-1, keepdims=True)
    byte = np.maximum(np.where(amax > 0, np.frexp(amax)[1] - 1 + 127, 0) - down, 1)
    scale = np.exp2(byte - 127.0)
    codes = (blocks / scale).astype(np.float32).astype(dtype).astype(np.float64)
    return np.moveaxis((codes * scale).reshape(v.shape), -1, axis)


WIDE = False


def mx_kscale(k):
    if not WIDE:
        return np.ones(k)
    levels = np.array([10, -10, 5, -5, 0])
    if k % 512:
        return np.exp2(np.random.permutation(np.resize(levels, k // 32))).repeat(32)
    a = np.empty((k // 512, 16))
    for p in range(k // 512):
        a[p, :8] = np.random.permutation(np.resize(levels, 8))
        for g in range(8):
            far = levels[np.abs(levels - a[p, g]) >= 10]
            a[p, g + 8] = far[np.random.randint(len(far))]
    return np.exp2(a.ravel()).repeat(32)


def f64(x):
    return np.asarray(x).astype(np.float64)


def striped(idx):
    return np.tile(idx.reshape(-1, 16).T, (8, 1)).astype(np.uint16)


def unstriped(offs):
    return offs[:16].T.reshape(-1).astype(np.int64)


def striped8(idx):
    return np.concatenate([x.reshape(-1, 16).T for x in idx]).astype(np.uint16)


def runs(offs, k):
    lists = np.stack([offs[16 * r : 16 * r + 16].T.reshape(-1) for r in range(8)]).astype(np.int64)
    return lists[np.arange(k) % 512 // 64]


def pack_weight(w):
    k, n = w.shape
    w = f64(np.asarray(w, np.float32).astype(ml_dtypes.bfloat16)).reshape(k // 32, 32, n)
    amax = np.abs(w).max(1)
    byte = np.clip(np.where(amax > 0, np.frexp(amax)[1] - 1 + 127 - 7, 1), 1, 254)
    scaled = (w * np.exp2(127.0 - byte)[:, None, :]).reshape(k, n).astype(np.float32)
    words = np.ascontiguousarray(scaled.reshape(k // 512, 128, 4, n).transpose(0, 1, 3, 2)).astype(ml_dtypes.float8_e4m3fn).view(np.uint8)
    return words, np.ascontiguousarray(byte.astype(np.uint8).reshape(k // 512, 16, n))


def unpack_weight(words, scales):
    g, p, n, _ = words.shape
    vals = np.ascontiguousarray(words).view(ml_dtypes.float8_e4m3fn).astype(np.float64) * np.repeat(np.exp2(scales.astype(np.float64) - 127.0), 8, axis=1)[..., None]
    return vals.transpose(0, 1, 3, 2).reshape(g * 512, n)


def sigmoid(v):
    return 1.0 / (1.0 + np.exp(-np.maximum(v, -700.0)))


K, T, S, N, H = 512, 2048, 512, 512, 512


def setup_inputs():
    n = np.random.standard_normal
    s = mx_kscale(K)[:, None]
    u = mx_kscale(H)
    packed_xT = pack_weight(n((K, T)) * s)
    return {
        "x_words": packed_xT[0],
        "x_scales": packed_xT[1],
        "w1": (n((K, H)) / np.sqrt(K) / s).astype(np.float32),
        "gn": (np.random.uniform(0.5, 1.5, (H, 1)) * u[:, None]).astype(np.float32),
        "w2": (n((H, N)) / np.sqrt(H) / u[:, None]).astype(np.float32),
        "offs": striped(np.random.permutation(T)[:S]),
        "n1": striped8(np.stack([np.random.permutation(S) for _ in range(8)])),
        "n2": striped8(np.stack([np.random.permutation(S) for _ in range(8)])),
        "n3": striped8(np.stack([np.random.permutation(S) for _ in range(8)])),
        "n4": striped8(np.stack([np.random.permutation(S) for _ in range(8)])),
        "n5": striped8(np.stack([np.random.permutation(S) for _ in range(8)])),
    }


def reference(x_words, x_scales, w1, gn, w2, offs, n1, n2, n3, n4, n5):
    xq = unpack_weight(x_words, x_scales)[:, unstriped(offs)]
    y = mxq(f64(w1), 0, "e4m3").T @ xq
    z = f64(gn) * (y * (sigmoid(y[np.arange(H)[:, None], runs(n1, H)])))
    h = mxq(f64(w2), 0, "e4m3").T @ mxq(z, 0, "e4m3")
    return np.maximum(h[np.arange(N)[:, None], runs(n2, N)] + y[np.arange(H)[:, None], runs(n4, H)], h[np.arange(N)[:, None], runs(n3, N)] + y[np.arange(H)[:, None], runs(n5, H)])

@@ -1,0 +1,186 @@
+from contextlib import ExitStack
+
+import concourse.mybir as mybir
+
+K, T, S, H, N = 512, 2048, 512, 512, 512
+FLOPS = 2 * K * H * S + 2 * H * N * S
+
+F32 = mybir.dt.float32
+BF16 = mybir.dt.bfloat16
+I32 = mybir.dt.int32
+U32 = mybir.dt.uint32
+U16 = mybir.dt.uint16
+U8 = mybir.dt.uint8
+FP8X4 = mybir.dt.float8_e4m3fn_x4
+ACT = mybir.ActivationFunctionType
+ALU = mybir.AluOpType
+
+P = 128
+PACK = 4
+WIN = 2 * S
+HALF = S // 2
+LCOLS = S // 16
+
+
+def tile_picked_skippathbgate_none_p_kernel(tc, x_words, x_scales, w1, gn, w2, offs, n1, n2, n3, n4, n5, out):
+    nc = tc.nc
+    with ExitStack() as ctx:
+        keep = ctx.enter_context(tc.tile_pool(name="keep", bufs=1))
+        psum = ctx.enter_context(tc.psum_pool(name="psum", bufs=1))
+
+        def list_tile(name):
+            return keep.tile([P, LCOLS], U16, name=name)
+
+        l_offs, l1, l2, l3, l4, l5 = [list_tile(x) for x in ("l_offs", "l1", "l2", "l3", "l4", "l5")]
+        xs = keep.tile([P, T], U8, align_bytes=64)
+        xw = keep.tile([P, T], I32, align_bytes=64)
+        warm = keep.tile([P, 2], F32)
+        gains = keep.tile([P, PACK], F32)
+        w1_raw = [keep.tile([P, PACK, H // 2], F32, name="w1_raw%d" % h) for h in range(2)]
+        w2_raw = keep.tile([P, PACK, N], F32)
+
+        nc.vector.memset(xs[:].bitcast(I32), 0)
+        nc.vector.memset(warm[:, 0:1], 0.0)
+        nc.scalar.activation(out=warm[:, 1:2], in_=warm[:, 0:1], func=ACT.Sigmoid)
+
+        nc.sync.dma_start(l_offs[:], offs)
+        w1_rows = w1.rearrange("(p j) c -> p j c", j=PACK)
+        w2_rows = w2.rearrange("(p j) c -> p j c", j=PACK)
+        for h in range(2):
+            nc.sync.dma_start(out=w1_raw[h][:], in_=w1_rows[:, :, h * 256 : (h + 1) * 256])
+        for q in range(4):
+            nc.sync.dma_start(out=xs[32 * q : 32 * q + 4, :].bitcast(I32), in_=x_scales[0, 4 * q : 4 * q + 4, :].bitcast(I32))
+        nc.sync.dma_start(out=xw[:], in_=x_words[0].rearrange("p n r -> p (n r)").bitcast(I32))
+        nc.sync.dma_start(l4[:], n4)
+        nc.sync.dma_start(l5[:], n5)
+        nc.sync.dma_start(l1[:], n1)
+        nc.sync.dma_start(out=gains[:], in_=gn.rearrange("(p t) o -> p (t o)", t=PACK))
+        nc.sync.dma_start(out=w2_raw[:], in_=w2_rows)
+        nc.sync.dma_start(l2[:], n2)
+        nc.sync.dma_start(l3[:], n3)
+
+        def deal(copy, grouped, raw, m0, m_lo, m_hi):
+            dst = grouped[:].rearrange("p (t m j) -> p m j t", t=PACK, j=PACK)[:, m0 + m_lo : m0 + m_hi]
+            src = raw[:].rearrange("p j (m t) -> p m j t", t=PACK)[:, m_lo:m_hi]
+            copy(out=dst, in_=src)
+
+        w1_g = keep.tile([P, H * PACK], BF16, align_bytes=64, tag="wg")
+        deal(nc.scalar.copy, w1_g, w1_raw[0], 0, 0, 64)
+        deal(nc.vector.tensor_copy, w1_g, w1_raw[1], 64, 0, 64)
+        xq_s = keep.tile([P, S], U8, align_bytes=64)
+        nc.vector.tensor_copy(out=xq_s[:], in_=xs[:].indirect(l_offs[:]))
+        w1_c = keep.tile([P, H], U32, align_bytes=64)
+        w1_s = keep.tile([P, H], U8, align_bytes=64)
+        nc.vector.quantize_mx(out=w1_c[:].bitcast(FP8X4), scales=w1_s[:], in_=w1_g[:])
+        xq_w = keep.tile([P, S], U32, align_bytes=64)
+
+        def half(u):
+            return slice(u * HALF, (u + 1) * HALF)
+
+        def half_list(lst, u):
+            return lst[:, u * LCOLS // 2 : (u + 1) * LCOLS // 2]
+
+        for u in range(2):
+            nc.vector.tensor_copy(out=xq_w[:, half(u)], in_=xw[:].bitcast(U32).indirect(half_list(l_offs, u)))
+
+        y_win = [keep.tile([P, WIN], F32, name="y_win%d" % t) for t in range(PACK)]
+        h_win = [keep.tile([P, WIN], F32, name="h_win%d" % t) for t in range(PACK)]
+
+        def product(name, t, u, w_c, w_s, a_c, a_s):
+            ps = psum.tile([P, HALF], F32, name="%s%d_%d" % (name, t, u), tag="bank%d_%d" % (t, u))
+            cols = slice(t * P, (t + 1) * P)
+            nc.tensor.matmul_mx(out=ps[:], lhsT=w_c[:, cols].bitcast(FP8X4), lhsT_scale=w_s[:, cols],
+                                rhs=a_c[:, half(u)].bitcast(FP8X4), rhs_scale=a_s[:, half(u)], start=True, stop=True)
+            return ps
+
+        y_ps = {}
+        for t in range(PACK):
+            for u in range(2):
+                y_ps[t, u] = product("y", t, u, w1_c, w1_s, xq_w, xq_s)
+                nc.scalar.copy(out=y_win[t][:, half(u)], in_=y_ps[t, u][:])
+
+        skip = {}
+
+        def fetch_skip(t, which, tag):
+            skip[t, which] = keep.tile([P, S], F32, name="skip%d_%d" % (t, which), tag=tag, align_bytes=64)
+            nc.vector.tensor_copy(out=skip[t, which][:], in_=y_win[t][:].indirect((l4, l5)[which][:]))
+
+        for t, which in ((0, 0), (0, 1), (1, 0), (1, 1), (2, 0)):
+            fetch_skip(t, which, "skip%d_%d" % (t, which))
+
+        z_c = keep.tile([P, S], U32, align_bytes=64)
+        z_s = keep.tile([P, S], U8, align_bytes=64)
+        w2_c = keep.tile([P, N], U32, align_bytes=64)
+        w2_s = keep.tile([P, N], U8, align_bytes=64)
+
+        def make_z(u):
+            yg = keep.tile([P, PACK, HALF], F32, name="yg%d" % u)
+            gate = keep.tile([P, PACK, HALF], F32, name="gate%d" % u)
+            for t in range(PACK):
+                nc.scalar.activation(out=yg[:, t, :], in_=y_ps[t, u][:], func=ACT.Copy, scale=gains[:, t : t + 1])
+                nc.scalar.activation(out=gate[:, t, :], in_=y_win[t][:].indirect(half_list(l1, u)), func=ACT.Sigmoid)
+            z_g = keep.tile([P, HALF * PACK], BF16, name="z_g%d" % u, tag="z_g%d" % u, align_bytes=64)
+            nc.vector.tensor_tensor(
+                out=z_g[:].rearrange("p (c i t) -> p c t i", i=4, t=PACK),
+                in0=yg[:].rearrange("p t (c i) -> p c t i", i=4),
+                in1=gate[:].rearrange("p t (c i) -> p c t i", i=4),
+                op=ALU.mult,
+            )
+            nc.vector.quantize_mx(out=z_c[:, half(u)].bitcast(FP8X4), scales=z_s[:, half(u)], in_=z_g[:])
+
+        def make_w2(v):
+            w2_g = keep.tile([P, 2 * P * PACK], BF16, name="w2_g%d" % v, tag="w2_g%d" % v, align_bytes=64)
+            nc.scalar.copy(
+                out=w2_g[:].rearrange("p (t m j) -> p m j t", t=2, j=PACK),
+                in_=w2_raw[:].rearrange("p j (m t) -> p m j t", t=PACK)[:, :, :, 2 * v : 2 * v + 2],
+            )
+            nc.vector.quantize_mx(out=w2_c[:, half(v)].bitcast(FP8X4), scales=w2_s[:, half(v)], in_=w2_g[:])
+
+        def make_h(t, u):
+            ps = product("h", t, u, w2_c, w2_s, z_c, z_s)
+            nc.scalar.copy(out=h_win[t][:, half(u)], in_=ps[:])
+
+        make_z(0)
+        fetch_skip(2, 1, "z_g0")
+        make_w2(0)
+        fetch_skip(3, 0, "w2_g0")
+        make_z(1)
+        make_h(0, 0)
+        make_h(1, 0)
+        make_w2(1)
+        make_h(0, 1)
+        make_h(1, 1)
+        fetch_skip(3, 1, "z_g1")
+        for t in (2, 3):
+            for u in range(2):
+                make_h(t, u)
+
+        out_rows = out.rearrange("(p t) s -> p t s", t=PACK)
+        sums = {}
+        for t in range(PACK):
+            for which in range(2):
+                sums[t, which] = keep.tile([P, S], F32, name="sum%d_%d" % (t, which))
+
+        def add_path(t, which):
+            nc.vector.tensor_tensor(out=sums[t, which][:], in0=h_win[t][:].indirect((l2, l3)[which][:]), in1=skip[t, which][:], op=ALU.add)
+
+        def add_path_half(t, which, u):
+            nc.vector.tensor_tensor(out=sums[t, which][:, half(u)], in0=h_win[t][:].indirect(half_list((l2, l3)[which], u)), in1=skip[t, which][:, half(u)], op=ALU.add)
+
+        def finish(t, cols, name):
+            res = keep.tile([P, cols.stop - cols.start], F32, name=name)
+            nc.vector.tensor_tensor(out=res[:], in0=sums[t, 0][:, cols], in1=sums[t, 1][:, cols], op=ALU.max)
+            nc.sync.dma_start(out=out_rows[:, t, cols], in_=res[:])
+
+        last = PACK - 1
+        for t in range(last):
+            add_path(t, 0)
+            if t > 0:
+                finish(t - 1, slice(0, S), "res%d" % (t - 1))
+            add_path(t, 1)
+        add_path(last, 0)
+        add_path_half(last, 1, 0)
+        finish(last - 1, slice(0, S), "res%d" % (last - 1))
+        add_path_half(last, 1, 1)
+        for u in range(2):
+            finish(last, half(u), "res_last%d" % u)

@@ -43,45 +43,44 @@ def tile_picked_skippathbgate_none_p_kernel(tc, x_words, x_scales, w1, gn, w2, o
         nc.vector.memset(warm[:, 0:1], 0.0)
         nc.scalar.activation(out=warm[:, 1:2], in_=warm[:, 0:1], func=ACT.Sigmoid)
 
-        nc.sync.dma_start(l_offs[:], offs)
         w1_rows = w1.rearrange("(p j) c -> p j c", j=PACK)
         w2_rows = w2.rearrange("(p j) c -> p j c", j=PACK)
-        for h in range(2):
-            nc.sync.dma_start(out=w1_raw[h][:], in_=w1_rows[:, :, h * 256 : (h + 1) * 256])
+        nc.sync.dma_start(out=xw[:], in_=x_words[0].rearrange("p n r -> p (n r)").bitcast(I32))
+        nc.sync.dma_start(l_offs[:], offs)
         for q in range(4):
             nc.sync.dma_start(out=xs[32 * q : 32 * q + 4, :].bitcast(I32), in_=x_scales[0, 4 * q : 4 * q + 4, :].bitcast(I32))
-        nc.sync.dma_start(out=xw[:], in_=x_words[0].rearrange("p n r -> p (n r)").bitcast(I32))
+        for h in range(2):
+            nc.sync.dma_start(out=w1_raw[h][:], in_=w1_rows[:, :, h * 256 : (h + 1) * 256])
         nc.sync.dma_start(l4[:], n4)
         nc.sync.dma_start(l5[:], n5)
-        nc.sync.dma_start(l1[:], n1)
         nc.sync.dma_start(out=gains[:], in_=gn.rearrange("(p t) o -> p (t o)", t=PACK))
+        nc.sync.dma_start(l1[:], n1)
         nc.sync.dma_start(out=w2_raw[:], in_=w2_rows)
         nc.sync.dma_start(l2[:], n2)
         nc.sync.dma_start(l3[:], n3)
 
-        def deal(copy, grouped, raw, m0, m_lo, m_hi):
-            dst = grouped[:].rearrange("p (t m j) -> p m j t", t=PACK, j=PACK)[:, m0 + m_lo : m0 + m_hi]
-            src = raw[:].rearrange("p j (m t) -> p m j t", t=PACK)[:, m_lo:m_hi]
-            copy(out=dst, in_=src)
-
-        w1_g = keep.tile([P, H * PACK], BF16, align_bytes=64, tag="wg")
-        deal(nc.scalar.copy, w1_g, w1_raw[0], 0, 0, 64)
-        deal(nc.vector.tensor_copy, w1_g, w1_raw[1], 64, 0, 64)
+        xq_w = keep.tile([P, S], U32, align_bytes=64)
+        nc.vector.tensor_copy(out=xq_w[:], in_=xw[:].bitcast(U32).indirect(l_offs[:]))
         xq_s = keep.tile([P, S], U8, align_bytes=64)
         nc.vector.tensor_copy(out=xq_s[:], in_=xs[:].indirect(l_offs[:]))
+
+        w1_g = [keep.tile([P, 2 * P * PACK], BF16, name="w1_g%d" % v, align_bytes=64) for v in range(2)]
+        for h, v, copy in ((0, 0, nc.scalar.copy), (0, 1, nc.scalar.copy), (1, 0, nc.vector.tensor_copy), (1, 1, nc.scalar.copy)):
+            copy(
+                out=w1_g[v][:].rearrange("p (t m j) -> p m j t", t=2, j=PACK)[:, 64 * h : 64 * h + 64],
+                in_=w1_raw[h][:].rearrange("p j (m t) -> p m j t", t=PACK)[:, :, :, 2 * v : 2 * v + 2],
+            )
         w1_c = keep.tile([P, H], U32, align_bytes=64)
         w1_s = keep.tile([P, H], U8, align_bytes=64)
-        nc.vector.quantize_mx(out=w1_c[:].bitcast(FP8X4), scales=w1_s[:], in_=w1_g[:])
-        xq_w = keep.tile([P, S], U32, align_bytes=64)
+        for t in range(PACK):
+            cols = slice(t * P, (t + 1) * P)
+            nc.vector.quantize_mx(out=w1_c[:, cols].bitcast(FP8X4), scales=w1_s[:, cols], in_=w1_g[t // 2][:, (t % 2) * 512 : (t % 2 + 1) * 512])
 
         def half(u):
             return slice(u * HALF, (u + 1) * HALF)
 
         def half_list(lst, u):
             return lst[:, u * LCOLS // 2 : (u + 1) * LCOLS // 2]
-
-        for u in range(2):
-            nc.vector.tensor_copy(out=xq_w[:, half(u)], in_=xw[:].bitcast(U32).indirect(half_list(l_offs, u)))
 
         y_win = [keep.tile([P, WIN], F32, name="y_win%d" % t) for t in range(PACK)]
         h_win = [keep.tile([P, WIN], F32, name="h_win%d" % t) for t in range(PACK)]
@@ -99,13 +98,17 @@ def tile_picked_skippathbgate_none_p_kernel(tc, x_words, x_scales, w1, gn, w2, o
                 y_ps[t, u] = product("y", t, u, w1_c, w1_s, xq_w, xq_s)
                 nc.scalar.copy(out=y_win[t][:, half(u)], in_=y_ps[t, u][:])
 
+        yg = keep.tile([P, PACK, S], F32)
+        for t in range(PACK):
+            nc.gpsimd.tensor_scalar(out=yg[:, t, :], in0=y_win[t][:, 0:S], scalar1=gains[:, t : t + 1], scalar2=0.0, op0=ALU.mult, op1=ALU.add)
+
         skip = {}
 
         def fetch_skip(t, which, tag):
             skip[t, which] = keep.tile([P, S], F32, name="skip%d_%d" % (t, which), tag=tag, align_bytes=64)
             nc.vector.tensor_copy(out=skip[t, which][:], in_=y_win[t][:].indirect((l4, l5)[which][:]))
 
-        for t, which in ((0, 0), (0, 1), (1, 0), (1, 1), (2, 0)):
+        for t, which in ((0, 0), (0, 1), (1, 0), (1, 1), (2, 0), (2, 1)):
             fetch_skip(t, which, "skip%d_%d" % (t, which))
 
         z_c = keep.tile([P, S], U32, align_bytes=64)
@@ -114,15 +117,13 @@ def tile_picked_skippathbgate_none_p_kernel(tc, x_words, x_scales, w1, gn, w2, o
         w2_s = keep.tile([P, N], U8, align_bytes=64)
 
         def make_z(u):
-            yg = keep.tile([P, PACK, HALF], F32, name="yg%d" % u)
             gate = keep.tile([P, PACK, HALF], F32, name="gate%d" % u)
             for t in range(PACK):
-                nc.scalar.activation(out=yg[:, t, :], in_=y_ps[t, u][:], func=ACT.Copy, scale=gains[:, t : t + 1])
                 nc.scalar.activation(out=gate[:, t, :], in_=y_win[t][:].indirect(half_list(l1, u)), func=ACT.Sigmoid)
             z_g = keep.tile([P, HALF * PACK], BF16, name="z_g%d" % u, tag="z_g%d" % u, align_bytes=64)
-            nc.vector.tensor_tensor(
+            (nc.gpsimd, nc.vector)[u].tensor_tensor(
                 out=z_g[:].rearrange("p (c i t) -> p c t i", i=4, t=PACK),
-                in0=yg[:].rearrange("p t (c i) -> p c t i", i=4),
+                in0=yg[:, :, half(u)].rearrange("p t (c i) -> p c t i", i=4),
                 in1=gate[:].rearrange("p t (c i) -> p c t i", i=4),
                 op=ALU.mult,
             )
@@ -141,7 +142,6 @@ def tile_picked_skippathbgate_none_p_kernel(tc, x_words, x_scales, w1, gn, w2, o
             nc.scalar.copy(out=h_win[t][:, half(u)], in_=ps[:])
 
         make_z(0)
-        fetch_skip(2, 1, "z_g0")
         make_w2(0)
         fetch_skip(3, 0, "w2_g0")
         make_z(1)

@@ -1,6 +1,7 @@
 from contextlib import ExitStack
 
 import concourse.mybir as mybir
+from concourse.masks import make_identity
 
 K, T, S, H, N = 512, 2048, 512, 512, 512
 FLOPS = 2 * K * H * S + 2 * H * N * S
@@ -82,105 +83,140 @@ def tile_picked_skippathbgate_none_p_kernel(tc, x_words, x_scales, w1, gn, w2, o
         def half_list(lst, u):
             return lst[:, u * LCOLS // 2 : (u + 1) * LCOLS // 2]
 
+        ident = keep.tile([P, P], F32)
+        make_identity(nc, ident[:])
         y_win = [keep.tile([P, WIN], F32, name="y_win%d" % t) for t in range(PACK)]
         h_win = [keep.tile([P, WIN], F32, name="h_win%d" % t) for t in range(PACK)]
 
-        def product(name, t, u, w_c, w_s, a_c, a_s):
-            ps = psum.tile([P, HALF], F32, name="%s%d_%d" % (name, t, u), tag="bank%d_%d" % (t, u))
-            cols = slice(t * P, (t + 1) * P)
-            nc.tensor.matmul_mx(out=ps[:], lhsT=w_c[:, cols].bitcast(FP8X4), lhsT_scale=w_s[:, cols],
-                                rhs=a_c[:, half(u)].bitcast(FP8X4), rhs_scale=a_s[:, half(u)], start=True, stop=True)
-            return ps
+        def bank(name, b):
+            return psum.tile([P, S], F32, name=name, tag="bank%d" % b)
 
-        y_ps = {}
+        def product(name, b, t, cols, w_c, w_s, a_c, a_s, win):
+            ps = bank(name, b)[:, 0 : cols.stop - cols.start]
+            nc.tensor.matmul_mx(out=ps, lhsT=w_c[:, t * P : (t + 1) * P].bitcast(FP8X4), lhsT_scale=w_s,
+                                rhs=a_c[:, cols].bitcast(FP8X4), rhs_scale=a_s[:, cols], start=True, stop=True)
+            nc.scalar.copy(out=win[:, cols], in_=ps)
+
         for t in range(PACK):
             for u in range(2):
-                y_ps[t, u] = product("y", t, u, w1_c, w1_s, xq_w, xq_s)
-                nc.scalar.copy(out=y_win[t][:, half(u)], in_=y_ps[t, u][:])
+                product("y%d_%d" % (t, u), 2 * t + u, t, half(u), w1_c, w1_s[:, t * P : (t + 1) * P], xq_w, xq_s, y_win[t])
 
         yg = keep.tile([P, PACK, S], F32)
         for t in range(PACK):
             nc.gpsimd.tensor_scalar(out=yg[:, t, :], in0=y_win[t][:, 0:S], scalar1=gains[:, t : t + 1], scalar2=0.0, op0=ALU.mult, op1=ALU.add)
 
-        skip = {}
+        def row(name, tag=None):
+            return keep.tile([P, S], F32, name=name, tag=tag or name, align_bytes=64)
 
-        def fetch_skip(t, which, tag):
-            skip[t, which] = keep.tile([P, S], F32, name="skip%d_%d" % (t, which), tag=tag, align_bytes=64)
-            nc.vector.tensor_copy(out=skip[t, which][:], in_=y_win[t][:].indirect((l4, l5)[which][:]))
+        def fetch(name, win, lst, tag=None):
+            got = row(name, tag)
+            nc.vector.tensor_copy(out=got[:], in_=win[:].indirect(lst[:]))
+            return got
 
-        for t, which in ((0, 0), (0, 1), (1, 0), (1, 1), (2, 0), (2, 1)):
-            fetch_skip(t, which, "skip%d_%d" % (t, which))
+        def fetch_op(got, win, lst, other, op):
+            nc.vector.tensor_tensor(out=got, in0=win[:].indirect(lst), in1=other, op=op)
 
-        z_c = keep.tile([P, S], U32, align_bytes=64)
+        y5 = {}
+        y4 = {}
+        y45 = {}
+        for t in range(2):
+            y5[t] = row("y5_%d" % t)
+            y45[t] = row("y45_%d" % t)
+            for u in range(2):
+                nc.vector.tensor_copy(out=y5[t][:, half(u)], in_=y_win[t][:].indirect(half_list(l5, u)))
+            for u in range(2):
+                fetch_op(y45[t][:, half(u)], y_win[t], half_list(l4, u), y5[t][:, half(u)], ALU.subtract)
+        y4[2] = fetch("y4_2", y_win[2], l4)
+        y5[2] = fetch("y5_2", y_win[2], l5)
+        y4[3] = fetch("y4_3", y_win[3], l4)
+
+        z_c = keep.tile([P, S], U32, name="z_codes", align_bytes=64)
         z_s = keep.tile([P, S], U8, align_bytes=64)
         w2_c = keep.tile([P, N], U32, align_bytes=64)
         w2_s = keep.tile([P, N], U8, align_bytes=64)
 
-        def make_z(u):
-            gate = keep.tile([P, PACK, HALF], F32, name="gate%d" % u)
+        gate = [keep.tile([P, PACK, HALF], F32, name="gate%d" % u, tag="gate%d" % u, align_bytes=64) for u in range(2)]
+        for u in range(2):
             for t in range(PACK):
-                nc.scalar.activation(out=gate[:, t, :], in_=y_win[t][:].indirect(half_list(l1, u)), func=ACT.Sigmoid)
-            z_g = keep.tile([P, HALF * PACK], BF16, name="z_g%d" % u, tag="z_g%d" % u, align_bytes=64)
-            (nc.gpsimd, nc.vector)[u].tensor_tensor(
+                nc.scalar.activation(out=gate[u][:, t, :], in_=y_win[t][:].indirect(half_list(l1, u)), func=ACT.Sigmoid)
+
+        def make_z(engine, u, lo, hi):
+            cols = slice(u * HALF + lo, u * HALF + hi)
+            z_g = keep.tile([P, (hi - lo) * PACK], BF16, name="z_g%d" % cols.start, align_bytes=64)
+            engine.tensor_tensor(
                 out=z_g[:].rearrange("p (c i t) -> p c t i", i=4, t=PACK),
-                in0=yg[:, :, half(u)].rearrange("p t (c i) -> p c t i", i=4),
-                in1=gate[:].rearrange("p t (c i) -> p c t i", i=4),
+                in0=yg[:, :, cols].rearrange("p t (c i) -> p c t i", i=4),
+                in1=gate[u][:, :, lo:hi].rearrange("p t (c i) -> p c t i", i=4),
                 op=ALU.mult,
             )
-            nc.vector.quantize_mx(out=z_c[:, half(u)].bitcast(FP8X4), scales=z_s[:, half(u)], in_=z_g[:])
+            return cols, z_g
 
-        def make_w2(v):
-            w2_g = keep.tile([P, 2 * P * PACK], BF16, name="w2_g%d" % v, tag="w2_g%d" % v, align_bytes=64)
+        z_parts = [make_z(nc.gpsimd, 0, 0, HALF), make_z(nc.vector, 1, 0, HALF // 2), make_z(nc.vector, 1, HALF // 2, HALF)]
+        w2_g = [keep.tile([P, 2 * P * PACK], BF16, name="w2_g%d" % v, align_bytes=64) for v in range(2)]
+        for v in range(2):
             nc.scalar.copy(
-                out=w2_g[:].rearrange("p (t m j) -> p m j t", t=2, j=PACK),
+                out=w2_g[v][:].rearrange("p (t m j) -> p m j t", t=2, j=PACK),
                 in_=w2_raw[:].rearrange("p j (m t) -> p m j t", t=PACK)[:, :, :, 2 * v : 2 * v + 2],
             )
-            nc.vector.quantize_mx(out=w2_c[:, half(v)].bitcast(FP8X4), scales=w2_s[:, half(v)], in_=w2_g[:])
 
-        def make_h(t, u):
-            ps = product("h", t, u, w2_c, w2_s, z_c, z_s)
-            nc.scalar.copy(out=h_win[t][:, half(u)], in_=ps[:])
+        def quantize_w2(v):
+            nc.vector.quantize_mx(out=w2_c[:, half(v)].bitcast(FP8X4), scales=w2_s[:, half(v)], in_=w2_g[v][:])
 
-        make_z(0)
-        make_w2(0)
-        fetch_skip(3, 0, "w2_g0")
-        make_z(1)
-        make_h(0, 0)
-        make_h(1, 0)
-        make_w2(1)
-        make_h(0, 1)
-        make_h(1, 1)
-        fetch_skip(3, 1, "z_g1")
-        for t in (2, 3):
+        def make_h(t, b, cols):
+            product("h%d_%d" % (t, b), b, t, cols, w2_c, w2_s[:, t * P : (t + 1) * P], z_c, z_s, h_win[t])
+
+        for cols, z_g in z_parts:
+            nc.vector.quantize_mx(out=z_c[:, cols].bitcast(FP8X4), scales=z_s[:, cols], in_=z_g[:])
+        quantize_w2(0)
+        quantize_w2(1)
+        y5[3] = fetch("y5_3", y_win[3], l5, "gate0")
+        for t in range(2):
             for u in range(2):
-                make_h(t, u)
+                make_h(t, 2 * t + u, half(u))
+        make_h(2, 4, slice(0, S))
+        make_h(3, 5, slice(0, S))
 
         out_rows = out.rearrange("(p t) s -> p t s", t=PACK)
-        sums = {}
-        for t in range(PACK):
-            for which in range(2):
-                sums[t, which] = keep.tile([P, S], F32, name="sum%d_%d" % (t, which))
+        lead = {t: row("lead%d" % t) for t in range(2)}
+        gap = {t: row("gap%d" % t) for t in range(2)}
+        for t in range(2):
+            fetch_op(lead[t][:], h_win[t], l2[:], y45[t][:], ALU.add)
+        for t in range(2):
+            fetch_op(gap[t][:], h_win[t], l3[:], lead[t][:], ALU.subtract)
 
-        def add_path(t, which):
-            nc.vector.tensor_tensor(out=sums[t, which][:], in0=h_win[t][:].indirect((l2, l3)[which][:]), in1=skip[t, which][:], op=ALU.add)
+        blocks = [slice(b * P, (b + 1) * P) for b in range(S // P)]
+        turned = {}
+        for t in range(2):
+            excess = row("excess%d" % t)
+            nc.scalar.activation(out=excess[:], in_=gap[t][:], func=ACT.Relu)
+            acc = bank("sum%d" % t, 6 + t)
+            terms = (y5[t], lead[t], excess)
+            for n, term in enumerate(terms):
+                for blk in blocks:
+                    nc.tensor.matmul(acc[:, blk], term[:, blk], ident[:], is_transpose=True,
+                                     start=(n == 0 and blk is blocks[0]), stop=(n == 2 and blk is blocks[-1]))
+            turned[t] = row("turned%d" % t)
+            nc.scalar.copy(out=turned[t][:], in_=acc[:])
+        for t in range(2):
+            back = bank("back%d" % t, t)
+            for blk in blocks:
+                nc.tensor.transpose(back[:, blk], turned[t][:, blk], ident[:])
+            res = row("res%d" % t)
+            nc.scalar.copy(out=res[:], in_=back[:])
+            nc.scalar.dma_start(out=out_rows[:, t, :], in_=res[:])
 
-        def add_path_half(t, which, u):
-            nc.vector.tensor_tensor(out=sums[t, which][:, half(u)], in0=h_win[t][:].indirect(half_list((l2, l3)[which], u)), in1=skip[t, which][:, half(u)], op=ALU.add)
+        sums = {(t, which): row("sum%d_%d" % (t, which)) for t in (2, 3) for which in range(2)}
 
         def finish(t, cols, name):
             res = keep.tile([P, cols.stop - cols.start], F32, name=name)
             nc.vector.tensor_tensor(out=res[:], in0=sums[t, 0][:, cols], in1=sums[t, 1][:, cols], op=ALU.max)
             nc.sync.dma_start(out=out_rows[:, t, cols], in_=res[:])
 
-        last = PACK - 1
-        for t in range(last):
-            add_path(t, 0)
-            if t > 0:
-                finish(t - 1, slice(0, S), "res%d" % (t - 1))
-            add_path(t, 1)
-        add_path(last, 0)
-        add_path_half(last, 1, 0)
-        finish(last - 1, slice(0, S), "res%d" % (last - 1))
-        add_path_half(last, 1, 1)
+        fetch_op(sums[2, 0][:], h_win[2], l2[:], y4[2][:], ALU.add)
+        fetch_op(sums[2, 1][:], h_win[2], l3[:], y5[2][:], ALU.add)
+        fetch_op(sums[3, 0][:], h_win[3], l2[:], y4[3][:], ALU.add)
+        finish(2, slice(0, S), "res2")
         for u in range(2):
-            finish(last, half(u), "res_last%d" % u)
+            fetch_op(sums[3, 1][:, half(u)], h_win[3], half_list(l3, u), y5[3][:, half(u)], ALU.add)
+        for u in range(2):
+            finish(3, half(u), "res3_%d" % u)

@@ -118,17 +118,10 @@ def tile_picked_skippathbgate_none_p_kernel(tc, x_words, x_scales, w1, gn, w2, o
 
         y5 = {}
         y4 = {}
-        y45 = {}
-        for t in range(2):
-            y5[t] = row("y5_%d" % t)
-            y45[t] = row("y45_%d" % t)
-            for u in range(2):
-                nc.vector.tensor_copy(out=y5[t][:, half(u)], in_=y_win[t][:].indirect(half_list(l5, u)))
-            for u in range(2):
-                fetch_op(y45[t][:, half(u)], y_win[t], half_list(l4, u), y5[t][:, half(u)], ALU.subtract)
-        y4[2] = fetch("y4_2", y_win[2], l4)
-        y5[2] = fetch("y5_2", y_win[2], l5)
-        y4[3] = fetch("y4_3", y_win[3], l4)
+        for t in range(PACK):
+            y5[t] = fetch("y5_%d" % t, y_win[t], l5)
+            if t > 0:
+                y4[t] = fetch("y4_%d" % t, y_win[t], l4)
 
         z_c = keep.tile([P, S], U32, name="z_codes", align_bytes=64)
         z_s = keep.tile([P, S], U8, align_bytes=64)
@@ -169,7 +162,8 @@ def tile_picked_skippathbgate_none_p_kernel(tc, x_words, x_scales, w1, gn, w2, o
             nc.vector.quantize_mx(out=z_c[:, cols].bitcast(FP8X4), scales=z_s[:, cols], in_=z_g[:])
         quantize_w2(0)
         quantize_w2(1)
-        y5[3] = fetch("y5_3", y_win[3], l5, "gate0")
+        y45 = row("y45", "gate0")
+        fetch_op(y45[:], y_win[0], l4[:], y5[0][:], ALU.subtract)
         for t in range(2):
             for u in range(2):
                 make_h(t, 2 * t + u, half(u))
@@ -177,44 +171,44 @@ def tile_picked_skippathbgate_none_p_kernel(tc, x_words, x_scales, w1, gn, w2, o
         make_h(3, 5, slice(0, S))
 
         out_rows = out.rearrange("(p t) s -> p t s", t=PACK)
-        lead = {t: row("lead%d" % t) for t in range(2)}
-        gap = {t: row("gap%d" % t) for t in range(2)}
-        for t in range(2):
-            fetch_op(lead[t][:], h_win[t], l2[:], y45[t][:], ALU.add)
-        for t in range(2):
-            fetch_op(gap[t][:], h_win[t], l3[:], lead[t][:], ALU.subtract)
+        sums = {(t, which): row("sum%d_%d" % (t, which)) for t in (1, 2, 3) for which in range(2)}
+        lead = row("lead")
+        gap = row("gap")
 
-        blocks = [slice(b * P, (b + 1) * P) for b in range(S // P)]
-        turned = {}
-        for t in range(2):
-            excess = row("excess%d" % t)
-            nc.scalar.activation(out=excess[:], in_=gap[t][:], func=ACT.Relu)
-            acc = bank("sum%d" % t, 6 + t)
-            terms = (y5[t], lead[t], excess)
-            for n, term in enumerate(terms):
-                for blk in blocks:
-                    nc.tensor.matmul(acc[:, blk], term[:, blk], ident[:], is_transpose=True,
-                                     start=(n == 0 and blk is blocks[0]), stop=(n == 2 and blk is blocks[-1]))
-            turned[t] = row("turned%d" % t)
-            nc.scalar.copy(out=turned[t][:], in_=acc[:])
-        for t in range(2):
-            back = bank("back%d" % t, t)
-            for blk in blocks:
-                nc.tensor.transpose(back[:, blk], turned[t][:, blk], ident[:])
-            res = row("res%d" % t)
-            nc.scalar.copy(out=res[:], in_=back[:])
-            nc.scalar.dma_start(out=out_rows[:, t, :], in_=res[:])
-
-        sums = {(t, which): row("sum%d_%d" % (t, which)) for t in (2, 3) for which in range(2)}
+        def add_path(t, which):
+            fetch_op(sums[t, which][:], h_win[t], (l2, l3)[which][:], (y4, y5)[which][t][:], ALU.add)
 
         def finish(t, cols, name):
             res = keep.tile([P, cols.stop - cols.start], F32, name=name)
             nc.vector.tensor_tensor(out=res[:], in0=sums[t, 0][:, cols], in1=sums[t, 1][:, cols], op=ALU.max)
             nc.sync.dma_start(out=out_rows[:, t, cols], in_=res[:])
 
-        fetch_op(sums[2, 0][:], h_win[2], l2[:], y4[2][:], ALU.add)
-        fetch_op(sums[2, 1][:], h_win[2], l3[:], y5[2][:], ALU.add)
-        fetch_op(sums[3, 0][:], h_win[3], l2[:], y4[3][:], ALU.add)
+        fetch_op(lead[:], h_win[0], l2[:], y45[:], ALU.add)
+        add_path(1, 0)
+        fetch_op(gap[:], h_win[0], l3[:], lead[:], ALU.subtract)
+        add_path(1, 1)
+
+        blocks = [slice(b * P, (b + 1) * P) for b in range(S // P)]
+        excess = row("excess")
+        nc.scalar.activation(out=excess[:], in_=gap[:], func=ACT.Relu)
+        acc = bank("acc", 6)
+        for n, term in enumerate((y5[0], lead, excess)):
+            for blk in blocks:
+                nc.tensor.matmul(acc[:, blk], term[:, blk], ident[:], is_transpose=True,
+                                 start=(n == 0 and blk is blocks[0]), stop=(n == 2 and blk is blocks[-1]))
+        turned = row("turned")
+        nc.scalar.copy(out=turned[:], in_=acc[:])
+        back = bank("back", 7)
+        for blk in blocks:
+            nc.tensor.transpose(back[:, blk], turned[:, blk], ident[:])
+        res0 = row("res0")
+        nc.scalar.copy(out=res0[:], in_=back[:])
+        nc.scalar.dma_start(out=out_rows[:, 0, :], in_=res0[:])
+
+        add_path(2, 0)
+        finish(1, slice(0, S), "res1")
+        add_path(2, 1)
+        add_path(3, 0)
         finish(2, slice(0, S), "res2")
         for u in range(2):
             fetch_op(sums[3, 1][:, half(u)], h_win[3], half_list(l3, u), y5[3][:, half(u)], ALU.add)

from contextlib import ExitStack

import concourse.mybir as mybir
from concourse.masks import make_identity

K, T, S, H, N = 512, 2048, 512, 512, 512
FLOPS = 2 * K * H * S + 2 * H * N * S

F32 = mybir.dt.float32
BF16 = mybir.dt.bfloat16
I32 = mybir.dt.int32
U32 = mybir.dt.uint32
U16 = mybir.dt.uint16
U8 = mybir.dt.uint8
FP8X4 = mybir.dt.float8_e4m3fn_x4
ACT = mybir.ActivationFunctionType
ALU = mybir.AluOpType

P = 128
PACK = 4
WIN = 2 * S
HALF = S // 2
LCOLS = S // 16


def tile_picked_skippathbgate_none_p_kernel(tc, x_words, x_scales, w1, gn, w2, offs, n1, n2, n3, n4, n5, out):
    nc = tc.nc
    with ExitStack() as ctx:
        keep = ctx.enter_context(tc.tile_pool(name="keep", bufs=1))
        psum = ctx.enter_context(tc.psum_pool(name="psum", bufs=1))

        def list_tile(name):
            return keep.tile([P, LCOLS], U16, name=name)

        l_offs, l1, l2, l3, l4, l5 = [list_tile(x) for x in ("l_offs", "l1", "l2", "l3", "l4", "l5")]
        xs = keep.tile([P, T], U8, align_bytes=64)
        xw = keep.tile([P, T], I32, align_bytes=64)
        warm = keep.tile([P, 2], F32)
        gains = keep.tile([P, PACK], F32)
        w1_raw = [keep.tile([P, PACK, H // 2], F32, name="w1_raw%d" % h) for h in range(2)]
        w2_raw = keep.tile([P, PACK, N], F32)

        nc.vector.memset(xs[:].bitcast(I32), 0)
        nc.vector.memset(warm[:, 0:1], 0.0)
        nc.scalar.activation(out=warm[:, 1:2], in_=warm[:, 0:1], func=ACT.Sigmoid)

        w1_rows = w1.rearrange("(p j) c -> p j c", j=PACK)
        w2_rows = w2.rearrange("(p j) c -> p j c", j=PACK)
        nc.sync.dma_start(out=xw[:], in_=x_words[0].rearrange("p n r -> p (n r)").bitcast(I32))
        nc.sync.dma_start(l_offs[:], offs)
        for q in range(4):
            nc.sync.dma_start(out=xs[32 * q : 32 * q + 4, :].bitcast(I32), in_=x_scales[0, 4 * q : 4 * q + 4, :].bitcast(I32))
        for h in range(2):
            nc.sync.dma_start(out=w1_raw[h][:], in_=w1_rows[:, :, h * 256 : (h + 1) * 256])
        nc.sync.dma_start(l4[:], n4)
        nc.sync.dma_start(l5[:], n5)
        nc.sync.dma_start(out=gains[:], in_=gn.rearrange("(p t) o -> p (t o)", t=PACK))
        nc.sync.dma_start(l1[:], n1)
        nc.sync.dma_start(out=w2_raw[:], in_=w2_rows)
        nc.sync.dma_start(l2[:], n2)
        nc.sync.dma_start(l3[:], n3)

        xq_w = keep.tile([P, S], U32, align_bytes=64)
        nc.vector.tensor_copy(out=xq_w[:], in_=xw[:].bitcast(U32).indirect(l_offs[:]))
        xq_s = keep.tile([P, S], U8, align_bytes=64)
        nc.vector.tensor_copy(out=xq_s[:], in_=xs[:].indirect(l_offs[:]))

        w1_g = [keep.tile([P, 2 * P * PACK], BF16, name="w1_g%d" % v, align_bytes=64) for v in range(2)]
        for h, v, copy in ((0, 0, nc.scalar.copy), (0, 1, nc.scalar.copy), (1, 0, nc.vector.tensor_copy), (1, 1, nc.scalar.copy)):
            copy(
                out=w1_g[v][:].rearrange("p (t m j) -> p m j t", t=2, j=PACK)[:, 64 * h : 64 * h + 64],
                in_=w1_raw[h][:].rearrange("p j (m t) -> p m j t", t=PACK)[:, :, :, 2 * v : 2 * v + 2],
            )
        w1_c = keep.tile([P, H], U32, align_bytes=64)
        w1_s = keep.tile([P, H], U8, align_bytes=64)
        for t in range(PACK):
            cols = slice(t * P, (t + 1) * P)
            nc.vector.quantize_mx(out=w1_c[:, cols].bitcast(FP8X4), scales=w1_s[:, cols], in_=w1_g[t // 2][:, (t % 2) * 512 : (t % 2 + 1) * 512])

        def half(u):
            return slice(u * HALF, (u + 1) * HALF)

        def half_list(lst, u):
            return lst[:, u * LCOLS // 2 : (u + 1) * LCOLS // 2]

        ident = keep.tile([P, P], F32)
        make_identity(nc, ident[:])
        y_win = [keep.tile([P, WIN], F32, name="y_win%d" % t) for t in range(PACK)]
        h_win = [keep.tile([P, WIN], F32, name="h_win%d" % t) for t in range(PACK)]

        def bank(name, b):
            return psum.tile([P, S], F32, name=name, tag="bank%d" % b)

        def product(name, b, t, cols, w_c, w_s, a_c, a_s, win):
            ps = bank(name, b)[:, 0 : cols.stop - cols.start]
            nc.tensor.matmul_mx(out=ps, lhsT=w_c[:, t * P : (t + 1) * P].bitcast(FP8X4), lhsT_scale=w_s,
                                rhs=a_c[:, cols].bitcast(FP8X4), rhs_scale=a_s[:, cols], start=True, stop=True)
            nc.scalar.copy(out=win[:, cols], in_=ps)

        for t in range(PACK):
            for u in range(2):
                product("y%d_%d" % (t, u), 2 * t + u, t, half(u), w1_c, w1_s[:, t * P : (t + 1) * P], xq_w, xq_s, y_win[t])

        yg = keep.tile([P, PACK, S], F32)
        for t in range(PACK):
            nc.gpsimd.tensor_scalar(out=yg[:, t, :], in0=y_win[t][:, 0:S], scalar1=gains[:, t : t + 1], scalar2=0.0, op0=ALU.mult, op1=ALU.add)

        def row(name, tag=None):
            return keep.tile([P, S], F32, name=name, tag=tag or name, align_bytes=64)

        def fetch(name, win, lst, tag=None):
            got = row(name, tag)
            nc.vector.tensor_copy(out=got[:], in_=win[:].indirect(lst[:]))
            return got

        def fetch_op(got, win, lst, other, op):
            nc.vector.tensor_tensor(out=got, in0=win[:].indirect(lst), in1=other, op=op)

        y5 = {}
        y4 = {}
        for t in range(PACK):
            y5[t] = fetch("y5_%d" % t, y_win[t], l5)
            if t > 0:
                y4[t] = fetch("y4_%d" % t, y_win[t], l4)

        z_c = keep.tile([P, S], U32, name="z_codes", align_bytes=64)
        z_s = keep.tile([P, S], U8, align_bytes=64)
        w2_c = keep.tile([P, N], U32, align_bytes=64)
        w2_s = keep.tile([P, N], U8, align_bytes=64)

        gate = [keep.tile([P, PACK, HALF], F32, name="gate%d" % u, tag="gate%d" % u, align_bytes=64) for u in range(2)]
        for u in range(2):
            for t in range(PACK):
                nc.scalar.activation(out=gate[u][:, t, :], in_=y_win[t][:].indirect(half_list(l1, u)), func=ACT.Sigmoid)

        def make_z(engine, u, lo, hi):
            cols = slice(u * HALF + lo, u * HALF + hi)
            z_g = keep.tile([P, (hi - lo) * PACK], BF16, name="z_g%d" % cols.start, align_bytes=64)
            engine.tensor_tensor(
                out=z_g[:].rearrange("p (c i t) -> p c t i", i=4, t=PACK),
                in0=yg[:, :, cols].rearrange("p t (c i) -> p c t i", i=4),
                in1=gate[u][:, :, lo:hi].rearrange("p t (c i) -> p c t i", i=4),
                op=ALU.mult,
            )
            return cols, z_g

        z_parts = [make_z(nc.gpsimd, 0, 0, HALF), make_z(nc.vector, 1, 0, HALF // 2), make_z(nc.vector, 1, HALF // 2, HALF)]
        w2_g = [keep.tile([P, 2 * P * PACK], BF16, name="w2_g%d" % v, align_bytes=64) for v in range(2)]
        for v in range(2):
            nc.scalar.copy(
                out=w2_g[v][:].rearrange("p (t m j) -> p m j t", t=2, j=PACK),
                in_=w2_raw[:].rearrange("p j (m t) -> p m j t", t=PACK)[:, :, :, 2 * v : 2 * v + 2],
            )

        def quantize_w2(v):
            nc.vector.quantize_mx(out=w2_c[:, half(v)].bitcast(FP8X4), scales=w2_s[:, half(v)], in_=w2_g[v][:])

        def make_h(t, b, cols):
            product("h%d_%d" % (t, b), b, t, cols, w2_c, w2_s[:, t * P : (t + 1) * P], z_c, z_s, h_win[t])

        for cols, z_g in z_parts:
            nc.vector.quantize_mx(out=z_c[:, cols].bitcast(FP8X4), scales=z_s[:, cols], in_=z_g[:])
        quantize_w2(0)
        quantize_w2(1)
        y45 = row("y45", "gate0")
        fetch_op(y45[:], y_win[0], l4[:], y5[0][:], ALU.subtract)
        for t in range(2):
            for u in range(2):
                make_h(t, 2 * t + u, half(u))
        make_h(2, 4, slice(0, S))
        make_h(3, 5, slice(0, S))

        out_rows = out.rearrange("(p t) s -> p t s", t=PACK)
        sums = {(t, which): row("sum%d_%d" % (t, which)) for t in (1, 2, 3) for which in range(2)}
        lead = row("lead")
        gap = row("gap")

        def add_path(t, which):
            fetch_op(sums[t, which][:], h_win[t], (l2, l3)[which][:], (y4, y5)[which][t][:], ALU.add)

        def finish(t, cols, name):
            res = keep.tile([P, cols.stop - cols.start], F32, name=name)
            nc.vector.tensor_tensor(out=res[:], in0=sums[t, 0][:, cols], in1=sums[t, 1][:, cols], op=ALU.max)
            nc.sync.dma_start(out=out_rows[:, t, cols], in_=res[:])

        fetch_op(lead[:], h_win[0], l2[:], y45[:], ALU.add)
        add_path(1, 0)
        fetch_op(gap[:], h_win[0], l3[:], lead[:], ALU.subtract)
        add_path(1, 1)

        blocks = [slice(b * P, (b + 1) * P) for b in range(S // P)]
        excess = row("excess")
        nc.scalar.activation(out=excess[:], in_=gap[:], func=ACT.Relu)
        acc = bank("acc", 6)
        for n, term in enumerate((y5[0], lead, excess)):
            for blk in blocks:
                nc.tensor.matmul(acc[:, blk], term[:, blk], ident[:], is_transpose=True,
                                 start=(n == 0 and blk is blocks[0]), stop=(n == 2 and blk is blocks[-1]))
        turned = row("turned")
        nc.scalar.copy(out=turned[:], in_=acc[:])
        back = bank("back", 7)
        for blk in blocks:
            nc.tensor.transpose(back[:, blk], turned[:, blk], ident[:])
        res0 = row("res0")
        nc.scalar.copy(out=res0[:], in_=back[:])
        nc.scalar.dma_start(out=out_rows[:, 0, :], in_=res0[:])

        add_path(2, 0)
        finish(1, slice(0, S), "res1")
        add_path(2, 1)
        add_path(3, 0)
        finish(2, slice(0, S), "res2")
        for u in range(2):
            fetch_op(sums[3, 1][:, half(u)], h_win[3], half_list(l3, u), y5[3][:, half(u)], ALU.add)
        for u in range(2):
            finish(3, half(u), "res3_%d" % u)
